import numpy as np
import ml_dtypes

BF16 = ml_dtypes.bfloat16


def bf(x):
    return np.asarray(x, np.float32).astype(BF16)


def f32(x):
    return np.asarray(x, np.float32)


def f64(x):
    return np.asarray(x).astype(np.float64)


def striped(idx):
    return np.tile(idx.reshape(-1, 16).T, (8, 1))


def rows(idx, k):
    return np.tile(idx, (k, 1))


def look(tab, idx):
    return np.take_along_axis(f64(tab), rows(idx, len(tab)), axis=1)


K, S, V, N, M = 128, 2048, 1024, 1024, 256


def setup_inputs():
    return {"tab": f32(np.random.standard_normal((2, K, S))), "th": f32(0.5 * np.random.standard_normal((K, V))), "w": bf(np.random.standard_normal((K, M)) / np.sqrt(K)), "b": f32(0.5 * np.random.standard_normal((M, 1))), "offs": striped(np.random.permutation(S)[:N])}


def reference(tab, th, w, b, offs):
    idx = offs[:16].T.reshape(-1)
    x = (look(tab[0], idx) >= f64(th)) * look(tab[1], idx)
    return np.maximum(f64(w).T @ x + f64(b), 0.0)

@@ -1,0 +1,60 @@
+import concourse.mybir as mybir
+
+F32, BF16, U16 = mybir.dt.float32, mybir.dt.bfloat16, mybir.dt.uint16
+ALU = mybir.AluOpType
+RELU = mybir.ActivationFunctionType.Relu
+
+P = 128
+S = 2048
+N = 1024
+M = 256
+PIECE = 512
+LANES = 16
+
+FLOPS = 2 * P * M * N
+
+
+def tile_lookup_sel_relu_kernel(tc, tab, th, w, b, offs, out):
+    nc = tc.nc
+    pieces = [slice(j, j + PIECE) for j in range(0, N, PIECE)]
+    blocks = [slice(m, m + P) for m in range(0, M, P)]
+
+    with (
+        tc.tile_pool(name="held", bufs=1) as held,
+        tc.tile_pool(name="work", bufs=2) as work,
+        tc.psum_pool(name="psum", bufs=4) as psum,
+    ):
+        offsets = held.tile([P, N // LANES], U16, name="offsets")
+        keys = held.tile([P, S], F32, name="keys")
+        values = held.tile([P, S], F32, name="values")
+        thresholds = held.tile([P, N], F32, name="thresholds")
+        mask = held.tile([P, N], F32, name="mask")
+        weights = held.tile([P, M], BF16, name="weights")
+        bias = [held.tile([P, 1], F32, name=f"bias{m}") for m in range(len(blocks))]
+
+        nc.sync.dma_start(offsets[:], offs)
+        nc.sync.dma_start(keys[:], tab[0])
+        for js in pieces:
+            nc.sync.dma_start(thresholds[:, js], th[:, js])
+        nc.sync.dma_start(values[:], tab[1])
+        nc.sync.dma_start(weights[:], w)
+        for m, rows in enumerate(blocks):
+            nc.sync.dma_start(bias[m][:], b[rows, :])
+
+        def entries(js):
+            return offsets[:, js.start // LANES : js.stop // LANES]
+
+        for js in pieces:
+            nc.vector.tensor_tensor(mask[:, js], keys[:].indirect(entries(js)), thresholds[:, js], ALU.is_ge)
+
+        for js in pieces:
+            picked = work.tile([P, PIECE], F32, name="picked")
+            nc.vector.tensor_tensor(picked[:], values[:].indirect(entries(js)), mask[:, js], ALU.mult)
+            x = work.tile([P, PIECE], BF16, name="x")
+            nc.scalar.copy(x[:], picked[:])
+            for m, rows in enumerate(blocks):
+                product = psum.tile([P, PIECE], F32, name="product")
+                nc.tensor.matmul(product[:], weights[:, rows], x[:], start=True, stop=True)
+                result = work.tile([P, PIECE], F32, name=f"result{m}")
+                nc.scalar.activation(result[:], product[:], RELU, bias=bias[m][:])
+                nc.sync.dma_start(out[rows, js], result[:])

@@ -8,7 +8,8 @@ P = 128
 S = 2048
 N = 1024
 M = 256
-PIECE = 512
+KEY_PIECE = 512
+PIECE = 256
 LANES = 16
 
 FLOPS = 2 * P * M * N
@@ -17,12 +18,13 @@ FLOPS = 2 * P * M * N
 def tile_lookup_sel_relu_kernel(tc, tab, th, w, b, offs, out):
     nc = tc.nc
     pieces = [slice(j, j + PIECE) for j in range(0, N, PIECE)]
+    key_pieces = [slice(j, j + KEY_PIECE) for j in range(0, N, KEY_PIECE)]
     blocks = [slice(m, m + P) for m in range(0, M, P)]
 
     with (
         tc.tile_pool(name="held", bufs=1) as held,
-        tc.tile_pool(name="work", bufs=2) as work,
-        tc.psum_pool(name="psum", bufs=4) as psum,
+        tc.tile_pool(name="work", bufs=4) as work,
+        tc.psum_pool(name="psum", bufs=8) as psum,
     ):
         offsets = held.tile([P, N // LANES], U16, name="offsets")
         keys = held.tile([P, S], F32, name="keys")
@@ -34,7 +36,7 @@ def tile_lookup_sel_relu_kernel(tc, tab, th, w, b, offs, out):
 
         nc.sync.dma_start(offsets[:], offs)
         nc.sync.dma_start(keys[:], tab[0])
-        for js in pieces:
+        for js in key_pieces:
             nc.sync.dma_start(thresholds[:, js], th[:, js])
         nc.sync.dma_start(values[:], tab[1])
         nc.sync.dma_start(weights[:], w)
@@ -44,17 +46,24 @@ def tile_lookup_sel_relu_kernel(tc, tab, th, w, b, offs, out):
         def entries(js):
             return offsets[:, js.start // LANES : js.stop // LANES]
 
-        for js in pieces:
+        for js in key_pieces:
             nc.vector.tensor_tensor(mask[:, js], keys[:].indirect(entries(js)), thresholds[:, js], ALU.is_ge)
 
         for js in pieces:
             picked = work.tile([P, PIECE], F32, name="picked")
             nc.vector.tensor_tensor(picked[:], values[:].indirect(entries(js)), mask[:, js], ALU.mult)
             x = work.tile([P, PIECE], BF16, name="x")
-            nc.scalar.copy(x[:], picked[:])
+            vector_free = js is pieces[-1]
+            if vector_free:
+                nc.vector.tensor_copy(x[:], picked[:])
+            else:
+                nc.scalar.copy(x[:], picked[:])
             for m, rows in enumerate(blocks):
                 product = psum.tile([P, PIECE], F32, name="product")
                 nc.tensor.matmul(product[:], weights[:, rows], x[:], start=True, stop=True)
                 result = work.tile([P, PIECE], F32, name=f"result{m}")
-                nc.scalar.activation(result[:], product[:], RELU, bias=bias[m][:])
+                if vector_free and m == 1:
+                    nc.vector.tensor_scalar(result[:], product[:], bias[m][:], 0.0, ALU.add, ALU.max)
+                else:
+                    nc.scalar.activation(result[:], product[:], RELU, bias=bias[m][:])
                 nc.sync.dma_start(out[rows, js], result[:])

@@ -53,16 +53,12 @@ def tile_lookup_sel_relu_kernel(tc, tab, th, w, b, offs, out):
             picked = work.tile([P, PIECE], F32, name="picked")
             nc.vector.tensor_tensor(picked[:], values[:].indirect(entries(js)), mask[:, js], ALU.mult)
             x = work.tile([P, PIECE], BF16, name="x")
-            vector_free = js is pieces[-1]
-            if vector_free:
-                nc.vector.tensor_copy(x[:], picked[:])
-            else:
-                nc.scalar.copy(x[:], picked[:])
+            nc.vector.tensor_copy(x[:], picked[:])
             for m, rows in enumerate(blocks):
                 product = psum.tile([P, PIECE], F32, name="product")
                 nc.tensor.matmul(product[:], weights[:, rows], x[:], start=True, stop=True)
                 result = work.tile([P, PIECE], F32, name=f"result{m}")
-                if vector_free and m == 1:
+                if js == pieces[-1] and m == 1:
                     nc.vector.tensor_scalar(result[:], product[:], bias[m][:], 0.0, ALU.add, ALU.max)
                 else:
                     nc.scalar.activation(result[:], product[:], RELU, bias=bias[m][:])

import concourse.mybir as mybir

F32, BF16, U16 = mybir.dt.float32, mybir.dt.bfloat16, mybir.dt.uint16
ALU = mybir.AluOpType
RELU = mybir.ActivationFunctionType.Relu

P = 128
S = 2048
N = 1024
M = 256
KEY_PIECE = 512
PIECE = 256
LANES = 16

FLOPS = 2 * P * M * N


def tile_lookup_sel_relu_kernel(tc, tab, th, w, b, offs, out):
    nc = tc.nc
    pieces = [slice(j, j + PIECE) for j in range(0, N, PIECE)]
    key_pieces = [slice(j, j + KEY_PIECE) for j in range(0, N, KEY_PIECE)]
    blocks = [slice(m, m + P) for m in range(0, M, P)]

    with (
        tc.tile_pool(name="held", bufs=1) as held,
        tc.tile_pool(name="work", bufs=4) as work,
        tc.psum_pool(name="psum", bufs=8) as psum,
    ):
        offsets = held.tile([P, N // LANES], U16, name="offsets")
        keys = held.tile([P, S], F32, name="keys")
        values = held.tile([P, S], F32, name="values")
        thresholds = held.tile([P, N], F32, name="thresholds")
        mask = held.tile([P, N], F32, name="mask")
        weights = held.tile([P, M], BF16, name="weights")
        bias = [held.tile([P, 1], F32, name=f"bias{m}") for m in range(len(blocks))]

        nc.sync.dma_start(offsets[:], offs)
        nc.sync.dma_start(keys[:], tab[0])
        for js in key_pieces:
            nc.sync.dma_start(thresholds[:, js], th[:, js])
        nc.sync.dma_start(values[:], tab[1])
        nc.sync.dma_start(weights[:], w)
        for m, rows in enumerate(blocks):
            nc.sync.dma_start(bias[m][:], b[rows, :])

        def entries(js):
            return offsets[:, js.start // LANES : js.stop // LANES]

        for js in key_pieces:
            nc.vector.tensor_tensor(mask[:, js], keys[:].indirect(entries(js)), thresholds[:, js], ALU.is_ge)

        for js in pieces:
            picked = work.tile([P, PIECE], F32, name="picked")
            nc.vector.tensor_tensor(picked[:], values[:].indirect(entries(js)), mask[:, js], ALU.mult)
            x = work.tile([P, PIECE], BF16, name="x")
            nc.vector.tensor_copy(x[:], picked[:])
            for m, rows in enumerate(blocks):
                product = psum.tile([P, PIECE], F32, name="product")
                nc.tensor.matmul(product[:], weights[:, rows], x[:], start=True, stop=True)
                result = work.tile([P, PIECE], F32, name=f"result{m}")
                if js == pieces[-1] and m == 1:
                    nc.vector.tensor_scalar(result[:], product[:], bias[m][:], 0.0, ALU.add, ALU.max)
                else:
                    nc.scalar.activation(result[:], product[:], RELU, bias=bias[m][:])
                nc.sync.dma_start(out[rows, js], result[:])
